import numpy as np
import ml_dtypes


def mxq(x, axis, fmt="e4m3"):
    dtype, down = {"e4m3": (ml_dtypes.float8_e4m3fn, 7), "e5m2": (ml_dtypes.float8_e5m2, 14)}[fmt]
    v = np.moveaxis(np.asarray(x, np.float32).astype(ml_dtypes.bfloat16).astype(np.float64), axis, -1)
    blocks = v.reshape(v.shape[:-1] + (-1, 32))
    amax = np.abs(blocks).max(-1, keepdims=True)
    byte = np.maximum(np.where(amax > 0, np.frexp(amax)[1] - 1 + 127, 0) - down, 1)
    scale = np.exp2(byte - 127.0)
    codes = (blocks / scale).astype(np.float32).astype(dtype).astype(np.float64)
    return np.moveaxis((codes * scale).reshape(v.shape), -1, axis)


WIDE = False


def mx_kscale(k):
    if not WIDE:
        return np.ones(k)
    levels = np.array([10, -10, 5, -5, 0])
    if k % 512:
        return np.exp2(np.random.permutation(np.resize(levels, k // 32))).repeat(32)
    a = np.empty((k // 512, 16))
    for p in range(k // 512):
        a[p, :8] = np.random.permutation(np.resize(levels, 8))
        for g in range(8):
            far = levels[np.abs(levels - a[p, g]) >= 10]
            a[p, g + 8] = far[np.random.randint(len(far))]
    return np.exp2(a.ravel()).repeat(32)


def f64(x):
    return np.asarray(x).astype(np.float64)


def striped(idx):
    return np.tile(np.asarray(idx).reshape(-1, 16).T, (8, 1)).astype(np.uint16)


def unstriped(offs):
    return offs[:16].T.reshape(-1).astype(np.int64)


E2M1 = np.array([0.0, 0.5, 1.0, 1.5, 2.0, 3.0, 4.0, 6.0, -0.0, -0.5, -1.0, -1.5, -2.0, -3.0, -4.0, -6.0])


def pack_weight(w, fmt):
    k, n = w.shape
    w = f64(np.asarray(w, np.float32).astype(ml_dtypes.bfloat16)).reshape(k // 32, 32, n)
    amax = np.abs(w).max(1)
    if fmt == "e4m3":
        byte = np.frexp(amax)[1] - 1 + 127 - 7
    else:
        mant, ex = np.frexp(amax / 6.0)
        byte = np.where(mant > 0.5, ex, ex - 1) + 127
    byte = np.clip(np.where(amax > 0, byte, 1), 1, 254)
    scaled = (w * np.exp2(127.0 - byte)[:, None, :]).reshape(k, n).astype(np.float32)
    by_word = np.ascontiguousarray(scaled.reshape(k // 512, 128, 4, n).transpose(0, 1, 3, 2))
    if fmt == "e4m3":
        words = by_word.astype(ml_dtypes.float8_e4m3fn).view(np.uint8)
    else:
        c = by_word.astype(ml_dtypes.float4_e2m1fn).view(np.uint8) & 0xF
        words = (c[..., 0::2] | (c[..., 1::2] << 4)).reshape(k // 512, 128, 2 * n)
    return np.ascontiguousarray(words), np.ascontiguousarray(byte.astype(np.uint8).reshape(k // 512, 16, n))


def unpack_weight(words, scales, fmt):
    g, _, n = scales.shape
    words = np.ascontiguousarray(words).reshape(g, 128, n, -1)
    if fmt == "e4m3":
        vals = words.view(ml_dtypes.float8_e4m3fn).astype(np.float64)
    else:
        nib = np.empty((g, 128, n, 4), np.uint8)
        nib[..., 0::2] = words & 0xF
        nib[..., 1::2] = words >> 4
        vals = E2M1[nib]
    vals = vals * np.repeat(np.exp2(scales.astype(np.float64) - 127.0), 8, axis=1)[..., None]
    return vals.transpose(0, 1, 3, 2).reshape(g * 512, n)


def sigmoid(v):
    return 1.0 / (1.0 + np.exp(-v))


def bf(x):
    return np.asarray(x, np.float32).astype(ml_dtypes.bfloat16)


def planes(Y):
    r, m = Y.shape
    b = f64(bf(Y)).reshape(r // 32, 32, m)
    amax = np.abs(b).max(1)
    byte = np.clip(np.where(amax > 0, np.frexp(amax)[1] - 1 + 127 - 7, 1), 1, 254)
    codes = (b * np.exp2(127.0 - byte)[:, None, :]).reshape(r, m).astype(np.float32).astype(ml_dtypes.float8_e4m3fn).view(np.uint8)
    words = codes.reshape(r // 512, 128, 4, m).transpose(0, 1, 3, 2)
    return np.ascontiguousarray(words), np.ascontiguousarray(byte.astype(np.uint8).reshape(r // 512, 16, m))


D, T, I, Q, E = 512, 2048, 512, 256, 512


def setup_inputs():
    n = np.random.standard_normal
    idx = np.random.permutation(T)[:I]
    idx4 = np.random.permutation(I)[:I]
    fd = mx_kscale(D)
    fi = mx_kscale(I)
    ti = np.ones(T)
    ti[idx] = fi
    keysp = pack_weight(n((D, T)) / fd[:, None], "e2m1")
    return {
        "query": (n((D, Q)) * 1.2 / np.sqrt(D) * fd[:, None]).astype(np.float32),
        "keys_words": keysp[0],
        "keys_scales": keysp[1],
        "guess": np.tile(np.random.uniform(0.05, 0.3, T), (128, 1)).astype(np.float32),
        "steep": np.tile(np.random.uniform(1.0, 3.0, T), (128, 1)).astype(np.float32),
        "thr": np.tile(np.random.uniform(-0.5, 1.0, T), (128, 1)).astype(np.float32),
        "lam": (np.random.uniform(0.6, 1.5, (Q, 1))).astype(np.float32),
        "pull": (np.random.uniform(0.4, 1.2, (Q, 1))).astype(np.float32),
        "os": (np.random.uniform(4.0, 16.0, (1, I)) * fi).astype(np.float32),
        "vals": (n((E, T)) / ti).astype(np.float32),
        "offs": striped(idx),
        "offs4": striped(idx4),
    }


def reference(query, keys_words, keys_scales, guess, steep, thr, lam, pull, os, vals, offs, offs4):
    idx = unstriped(offs)
    idx4 = unstriped(offs4)
    keysu = unpack_weight(keys_words, keys_scales, "e2m1")
    queryq = mxq(f64(query), 0, "e4m3")
    keysidxg = keysu[:, idx]
    a = queryq.T @ keysidxg
    sg = sigmoid((a - f64(thr)[:1][:, idx]) * f64(steep)[:1][:, idx])
    s = np.log(sg * (1.0 - f64(guess)[:1][:, idx]) + f64(guess)[:1][:, idx]) * f64(lam)
    p = np.exp(s - np.max(s, axis=1, keepdims=True))
    r = p / np.sum(p, axis=1, keepdims=True)
    w = r + r[:, idx4] * f64(pull)
    wo1 = w * f64(os)
    wt1 = wo1.T
    vt1 = f64(vals)[:, idx].T
    vt1q = mxq(vt1, 0, "e4m3")
    wt1q = mxq(wt1, 0, "e4m3")
    o = vt1q.T @ wt1q
    words, scales = planes(o)
    return o, words, scales

from contextlib import ExitStack

import concourse.mybir as mybir
from concourse.masks import make_identity

D, T, I, Q, E = 512, 2048, 512, 256, 512
FLOPS = 2 * D * Q * I + 2 * I * E * Q

F32 = mybir.dt.float32
BF16 = mybir.dt.bfloat16
I32 = mybir.dt.int32
U32 = mybir.dt.uint32
U16 = mybir.dt.uint16
U8 = mybir.dt.uint8
FP8X4 = mybir.dt.float8_e4m3fn_x4
FP4X4 = mybir.dt.float4_e2m1fn_x4
ALU = mybir.AluOpType
ACT = mybir.ActivationFunctionType

P = 128
LAST = P - 1
HALF = I // 2


def tile_attend_answerodds_followed_read_pl_kernel(
    tc, query, keys_words, keys_scales, guess, steep, thr, lam, pull, factor, vals, offs, offs4, out_0, out_1, out_2
):
    nc = tc.nc
    with ExitStack() as ctx:
        keep = ctx.enter_context(tc.tile_pool(name="keep", bufs=1))
        psum = ctx.enter_context(tc.psum_pool(name="psum", bufs=1))

        def sb(name, shape, dtype, tag=None):
            return keep.tile(shape, dtype, name=name, tag=tag or name, align_bytes=64)

        def bank(tag, shape):
            return psum.tile(shape, F32, name=tag, tag=tag)

        def quantize(codes, scales, values):
            nc.vector.quantize_mx(out=codes.bitcast(FP8X4), scales=scales, in_=values)

        idx = keep.tile([P, I // 16], U16, name="idx")
        idx4 = keep.tile([P, I // 16], U16, name="idx4")
        thr_w = sb("thr_w", [P, T], F32)
        steep_w = sb("steep_w", [P, T], F32)
        guess_w = sb("guess_w", [P, T], F32)
        kw_w = sb("kw_w", [P, T], U16)
        ks_w = sb("ks_w", [P, T], U8)
        q_raw = sb("q_raw", [P, 4, Q], F32)
        v_w = [sb("v_w%d" % j, [P, T], F32) for j in range(4)]
        ident = sb("ident", [P, P], F32)
        lam_c = sb("lam_c", [P, 2], F32)
        pull_c = sb("pull_c", [P, 2], F32)
        os_c = sb("os_c", [P, 4], F32)

        nc.gpsimd.memset(ks_w[:].bitcast(I32), 0)
        nc.vector.memset(thr_w[0:LAST, 0 : T - 1], 0.0)
        nc.vector.memset(thr_w[0:LAST, T - 1 : T], 0.0)
        make_identity(nc, ident[:])
        nc.gpsimd.memset(steep_w[0:LAST, :], 0.0)
        nc.gpsimd.memset(guess_w[0:LAST, :], 0.0)

        vals_dealt = vals.rearrange("(p j) t -> j p t", j=4)
        nc.sync.dma_start(idx[:], offs)
        nc.sync.dma_start(thr_w[LAST:P, :], thr[0:1, :])
        nc.sync.dma_start(steep_w[LAST:P, :], steep[0:1, :])
        nc.sync.dma_start(q_raw[:], query.rearrange("(p j) q -> p j q", j=4))
        nc.sync.dma_start(kw_w[:].bitcast(I32), keys_words[0].bitcast(I32))
        for quad in range(4):
            nc.sync.dma_start(
                ks_w[32 * quad : 32 * quad + 4, :].bitcast(I32),
                keys_scales[0, 4 * quad : 4 * quad + 4, :].bitcast(I32),
            )
        nc.sync.dma_start(guess_w[LAST:P, :], guess[0:1, :])
        nc.sync.dma_start(v_w[0][:], vals_dealt[0])
        nc.sync.dma_start(idx4[:], offs4)
        with nc.allow_non_contiguous_dma(reason="one number a partition"):
            nc.sync.dma_start(lam_c[:], lam.rearrange("(h p) one -> p (h one)", h=2))
            nc.sync.dma_start(pull_c[:], pull.rearrange("(h p) one -> p (h one)", h=2))
        nc.sync.dma_start(os_c[:], factor.rearrange("one (p t) -> (one p) t", t=4))
        nc.sync.dma_start(v_w[1][:], vals_dealt[1])
        nc.sync.dma_start(v_w[2][:], vals_dealt[2])
        nc.sync.dma_start(v_w[3][:], vals_dealt[3])

        warm = sb("warm", [P, 1], F32)
        nc.scalar.activation(warm[:], ident[:, 0:1], ACT.Sigmoid)

        def gather_turn(window, name, tag):
            g = sb(name, [P, I], F32)
            nc.vector.tensor_copy(g[:], window[:].indirect(idx[:]))
            ps = bank(tag, [P, 4, P])
            for b in range(4):
                nc.tensor.transpose(ps[:, b, :], g[:, b * P : (b + 1) * P], ident[:])
            return ps

        q_bf = sb("q_bf", [P, Q, 4], BF16)
        q_c = sb("q_c", [P, Q], U32)
        q_s = sb("q_s", [P, Q], U8)
        nc.scalar.copy(q_bf[:], q_raw[:].rearrange("p j q -> p q j"))

        thr_ps = gather_turn(thr_w, "thr_g", "A")
        steep_ps = gather_turn(steep_w, "steep_g", "B")
        quantize(q_c[:], q_s[:], q_bf[:].rearrange("p q j -> p (q j)"))

        steep_c = sb("steep_c", [P, 4], F32)
        neg_steep_c = sb("neg_steep_c", [P, 4], F32)
        bias_c = sb("bias_c", [P, 4], F32)
        nc.scalar.activation(neg_steep_c[:], steep_ps[:, :, LAST], ACT.Copy, scale=-1.0)
        nc.scalar.copy(steep_c[:], steep_ps[:, :, LAST])
        for b in range(4):
            nc.scalar.activation(bias_c[:, b : b + 1], thr_ps[:, b, LAST:P], ACT.Copy, scale=neg_steep_c[:, b : b + 1])

        sc = [bank("D", [P, 2, Q]), bank("E", [P, 2, Q])]
        sg = sb("sg", [P, 4, Q], F32)
        for half in range(2):
            kw_g = sb("kw_g%d" % half, [P, HALF], U16)
            ks_g = sb("ks_g%d" % half, [P, HALF], U8)
            entries = idx[:, half * 16 : (half + 1) * 16]
            nc.vector.tensor_copy(kw_g[:], kw_w[:].indirect(entries))
            nc.vector.tensor_copy(ks_g[:], ks_w[:].indirect(entries))
            for c in range(2):
                cols = slice(c * P, (c + 1) * P)
                nc.tensor.matmul_mx(
                    out=sc[half][:, c, :],
                    lhsT=kw_g[:, cols].bitcast(FP4X4),
                    lhsT_scale=ks_g[:, cols],
                    rhs=q_c[:].bitcast(FP8X4),
                    rhs_scale=q_s[:],
                    start=True,
                    stop=True,
                )
            for c in range(2):
                b = 2 * half + c
                nc.scalar.activation(
                    sg[:, b, :], sc[half][:, c, :], ACT.Sigmoid, bias=bias_c[:, b : b + 1], scale=steep_c[:, b : b + 1]
                )

        guess_ps = gather_turn(guess_w, "guess_g", "C")

        v_g = [sb("v_g%d" % j, [P, I], BF16) for j in range(4)]
        v_ps = [bank("F", [P, 2, 2, P]), bank("G", [P, 2, 2, P])]

        def gather_values(j):
            nc.vector.tensor_copy(v_g[j][:], v_w[j][:].indirect(idx[:]))
            words = v_g[j][:].bitcast(F32)
            for u in range(2):
                nc.tensor.transpose(v_ps[j // 2][:, j % 2, u, :], words[:, u:HALF:2], ident[:])

        gather_values(0)
        guess_c = sb("guess_c", [P, 2, 4], F32, tag="v_w0")
        nc.vector.tensor_copy(guess_c[:, 0, :], guess_ps[:, :, LAST])
        nc.vector.tensor_scalar(guess_c[:, 1, :], guess_ps[:, :, LAST], -1.0, 1.0, ALU.mult, ALU.add)

        lnc = sb("lnc", [P, 4, Q], F32)
        lnc_t = [bank("A", [P, I]), bank("B", [P, I])]
        for b in range(4):
            nc.scalar.activation(
                lnc[:, b, :], sg[:, b, :], ACT.Ln, bias=guess_c[:, 0, b : b + 1], scale=guess_c[:, 1, b : b + 1]
            )
            for h in range(2):
                nc.tensor.transpose(lnc_t[h][:, b * P : (b + 1) * P], lnc[:, b, h * P : (h + 1) * P], ident[:])

        neg_lam = sb("neg_lam", [P, 2], F32)
        nc.scalar.activation(neg_lam[:], lam_c[:], ACT.Copy, scale=-1.0)

        gather_values(1)
        gather_values(2)

        p = [sb("p%d" % h, [P, I], F32) for h in range(2)]
        r = [sb("r%d" % h, [P, I], F32) for h in range(2)]
        neg_s = sb("neg_s", [P, 2, I], F32, tag="v_w2")
        low = [sb("low%d" % h, [P, 1], F32) for h in range(2)]
        total = [sb("total%d" % h, [P, 1], F32) for h in range(2)]
        inv = [sb("inv%d" % h, [P, 1], F32) for h in range(2)]
        for h in range(2):
            nc.vector.tensor_scalar(
                neg_s[:, h, :], lnc_t[h][:], neg_lam[:, h : h + 1], None, ALU.mult, ALU.min, accum_out=low[h][:]
            )
            nc.scalar.activation(p[h][:], neg_s[:, h, :], ACT.Exp, bias=low[h][:], scale=-1.0, accum_out=total[h][:])
        for h in range(2):
            nc.vector.reciprocal(inv[h][:], total[h][:])
            nc.scalar.activation(r[h][:], p[h][:], ACT.Copy, scale=inv[h][:])
        gather_values(3)

        w_ps = [bank("D", [P, 4, P]), bank("E", [P, 4, P])]
        for h in range(2):
            r_g = sb("r_g%d" % h, [P, I], F32, tag="v_w3" if h == 0 else None)
            pulled = sb("pulled%d" % h, [P, I], F32)
            for half in range(2):
                cols = slice(half * HALF, (half + 1) * HALF)
                nc.vector.tensor_copy(r_g[:, cols], r[h][:].indirect(idx4[:, half * 16 : (half + 1) * 16]))
                nc.scalar.activation(pulled[:, cols], r_g[:, cols], ACT.Copy, scale=pull_c[:, h : h + 1])
            for n, src in enumerate((r[h], pulled)):
                for t in range(4):
                    nc.tensor.matmul(
                        w_ps[h][:, t, :],
                        lhsT=src[:, t:I:4],
                        rhs=ident[:],
                        start=(n == 0 and t == 0),
                        stop=(n == 1 and t == 3),
                        is_transpose=True,
                    )

        v_bf = sb("v_bf", [P, 4, P, 4], BF16, tag="v_w2")
        v_c = sb("v_c", [P, 4, P], U32)
        v_s = sb("v_s", [P, 4, P], U8)
        for pair in range(2):
            js = slice(2 * pair, 2 * pair + 2)
            nc.scalar.copy(v_bf[:, js, :, :].bitcast(F32), v_ps[pair][:].rearrange("p j u e -> p j e u"))
            quantize(
                v_c[:, js, :].rearrange("p j e -> p (j e)"),
                v_s[:, js, :].rearrange("p j e -> p (j e)"),
                v_bf[:, js, :, :].rearrange("p j e t -> p (j e t)"),
            )

        os_b = os_c[:].unsqueeze(1).to_broadcast([P, P, 4])
        o_c = sb("o_c", [P, Q], U32)
        o_s = sb("o_s", [P, Q], U8)
        out_dealt = out_0.rearrange("(p j) q -> p j q", j=4)
        out_words = out_1[0].rearrange("p c r -> p (c r)").bitcast(I32)
        o_ps = [bank("H", [P, 4, P]), bank("C", [P, 4, P])]
        for h in range(2):
            w_bf = sb("w_bf%d" % h, [P, P, 4], BF16)
            w_c = sb("w_c%d" % h, [P, P], U32)
            w_s = sb("w_s%d" % h, [P, P], U8)
            nc.vector.tensor_tensor(w_bf[:], w_ps[h][:].rearrange("p t q -> p q t"), os_b, ALU.mult)
            quantize(w_c[:], w_s[:], w_bf[:].rearrange("p q t -> p (q t)"))
            for j in range(4):
                nc.tensor.matmul_mx(
                    out=o_ps[h][:, j, :],
                    lhsT=v_c[:, j, :].bitcast(FP8X4),
                    lhsT_scale=v_s[:, j, :],
                    rhs=w_c[:].bitcast(FP8X4),
                    rhs_scale=w_s[:],
                    start=True,
                    stop=True,
                )
        for h in range(2):
            qs = slice(h * P, (h + 1) * P)
            o_bf = sb("o_bf%d" % h, [P, P, 4], BF16)
            o_f = sb("o_f%d" % h, [P, 4, P], F32)
            if h == 0:
                nc.scalar.copy(o_bf[:], o_ps[h][:].rearrange("p j q -> p q j"))
            else:
                nc.vector.tensor_copy(o_bf[:], o_ps[h][:].rearrange("p j q -> p q j"))
            nc.scalar.copy(o_f[:], o_ps[h][:])
            quantize(o_c[:, qs], o_s[:, qs], o_bf[:].rearrange("p q j -> p (q j)"))
            nc.sync.dma_start(out_dealt[:, :, qs], o_f[:])
            nc.sync.dma_start(out_words[:, qs], o_c[:, qs].bitcast(I32))
        for quad in range(4):
            queue = nc.sync if quad % 2 else nc.scalar
            queue.dma_start(
                out_2[0, 4 * quad : 4 * quad + 4, :].bitcast(I32), o_s[32 * quad : 32 * quad + 4, :].bitcast(I32)
            )
